import numpy as np
import ml_dtypes

BF16 = ml_dtypes.bfloat16


def bf(x):
    return np.asarray(x, np.float32).astype(BF16)


def f32(x):
    return np.asarray(x, np.float32)


def f64(x):
    return np.asarray(x).astype(np.float64)


def striped(idx):
    return np.tile(idx.reshape(-1, 16).T, (8, 1))


S, K, M, N, E, Q = 512, 128, 256, 256, 2, 128


def gelu_tanh(v):
    return 0.5 * v * (1.0 + np.tanh(np.sqrt(2.0 / np.pi) * (v + 0.044715 * v**3)))


def setup_inputs():
    return {"base": bf(np.random.standard_normal((M, S))), "x": bf(np.random.standard_normal((K, N))), "w": bf(np.random.standard_normal((E, K, M)) / np.sqrt(K)), "b": f32(0.5 * np.random.standard_normal((M, 1))), "offs": striped(np.random.permutation(S)[:N])}


def reference(base, x, w, b, offs):
    idx = offs[:16].T.reshape(-1)
    z = f64(base).copy()
    for e in range(E):
        z[:, idx[e * Q : (e + 1) * Q]] += f64(w)[e].T @ f64(x)[:, e * Q : (e + 1) * Q]
    return gelu_tanh(z + f64(b))

@@ -1,0 +1,62 @@
+import concourse.mybir as mybir
+from concourse.masks import make_identity
+
+BF16 = mybir.dt.bfloat16
+F32 = mybir.dt.float32
+U16 = mybir.dt.uint16
+GELU = mybir.ActivationFunctionType.Gelu_apprx_tanh
+
+P = 128
+PER_COLUMN = 16
+
+FLOPS = 2 * 128 * 256 * 256
+
+
+def tile_scatter_matmul_kernel(tc, base, x, w, b, offs, out):
+    nc = tc.nc
+    features, tokens = base.shape
+    contraction, entries = x.shape
+    experts = w.shape[0]
+    piece = entries // experts
+    blocks = features // P
+    assert contraction == P
+
+    with (
+        tc.tile_pool(name="held", bufs=1) as held,
+        tc.psum_pool(name="banks", bufs=1) as banks,
+    ):
+        offsets = held.tile([P, entries // PER_COLUMN], U16, name="offsets")
+        nc.sync.dma_start(offsets[:], offs)
+
+        identity = held.tile([P, P], BF16, name="identity")
+        make_identity(nc, identity[:])
+        base_rows = [held.tile([P, tokens], BF16, name=f"base_rows{a}") for a in range(blocks)]
+        nc.sync.dma_start(base_rows[0][:], base[0:P, :])
+        nc.scalar.dma_start(base_rows[1][:], base[P : 2 * P, :])
+        moving = held.tile([P, entries], BF16, name="moving")
+        nc.sync.dma_start(moving[:], x)
+        weights = held.tile([P, experts, features], BF16, name="weights")
+        nc.scalar.dma_start(weights[:], w.rearrange("e k m -> k e m"))
+        bias = held.tile([P, blocks], F32, name="bias")
+        with nc.allow_non_contiguous_dma(reason="one float32 of the bias to a partition and block"):
+            nc.scalar.dma_start(bias[:], b.rearrange("(a p) o -> p (a o)", p=P))
+
+        windows = [banks.tile([P, tokens], F32, name=f"window{a}") for a in range(blocks)]
+        for a in range(blocks):
+            nc.tensor.matmul(windows[a][:], identity[:], base_rows[a][:], start=True, stop=False)
+
+        for a in range(blocks):
+            for e in range(experts):
+                columns = piece // PER_COLUMN
+                nc.tensor.matmul(
+                    windows[a][:].indirect(offsets[:, e * columns : (e + 1) * columns]),
+                    weights[:, e, a * P : (a + 1) * P],
+                    moving[:, e * piece : (e + 1) * piece],
+                    start=False,
+                    stop=(e == experts - 1),
+                )
+
+        for a in range(blocks):
+            result = held.tile([P, tokens], F32, name=f"result{a}")
+            nc.scalar.activation(result[:], windows[a][:], GELU, bias=bias[:, a : a + 1])
+            nc.sync.dma_start(out[a * P : (a + 1) * P, :], result[:])

@@ -25,14 +25,13 @@ def tile_scatter_matmul_kernel(tc, base, x, w, b, offs, out):
         tc.tile_pool(name="held", bufs=1) as held,
         tc.psum_pool(name="banks", bufs=1) as banks,
     ):
-        offsets = held.tile([P, entries // PER_COLUMN], U16, name="offsets")
-        nc.sync.dma_start(offsets[:], offs)
-
         identity = held.tile([P, P], BF16, name="identity")
         make_identity(nc, identity[:])
         base_rows = [held.tile([P, tokens], BF16, name=f"base_rows{a}") for a in range(blocks)]
         nc.sync.dma_start(base_rows[0][:], base[0:P, :])
         nc.scalar.dma_start(base_rows[1][:], base[P : 2 * P, :])
+        offsets = held.tile([P, entries // PER_COLUMN], U16, name="offsets")
+        nc.sync.dma_start(offsets[:], offs)
         moving = held.tile([P, entries], BF16, name="moving")
         nc.sync.dma_start(moving[:], x)
         weights = held.tile([P, experts, features], BF16, name="weights")
@@ -40,6 +39,10 @@ def tile_scatter_matmul_kernel(tc, base, x, w, b, offs, out):
         bias = held.tile([P, blocks], F32, name="bias")
         with nc.allow_non_contiguous_dma(reason="one float32 of the bias to a partition and block"):
             nc.scalar.dma_start(bias[:], b.rearrange("(a p) o -> p (a o)", p=P))
+
+        scratch = held.tile([P, 1], F32, name="scratch")
+        nc.vector.memset(scratch[:], 0.0)
+        nc.scalar.activation(scratch[:], scratch[:], GELU)
 
         windows = [banks.tile([P, tokens], F32, name=f"window{a}") for a in range(blocks)]
         for a in range(blocks):

@@ -9,6 +9,8 @@ GELU = mybir.ActivationFunctionType.Gelu_apprx_tanh
 P = 128
 PER_COLUMN = 16
 
+WARM_UPS = 16
+
 FLOPS = 2 * 128 * 256 * 256
 
 
@@ -18,6 +20,7 @@ def tile_scatter_matmul_kernel(tc, base, x, w, b, offs, out):
     contraction, entries = x.shape
     experts = w.shape[0]
     piece = entries // experts
+    piece_columns = piece // PER_COLUMN
     blocks = features // P
     assert contraction == P
 
@@ -25,6 +28,12 @@ def tile_scatter_matmul_kernel(tc, base, x, w, b, offs, out):
         tc.tile_pool(name="held", bufs=1) as held,
         tc.psum_pool(name="banks", bufs=1) as banks,
     ):
+        zeros = held.tile([P, P], BF16, name="zeros")
+        nc.vector.memset(zeros[:], 0.0)
+        unread = banks.tile([P, P], F32, name="unread")
+        for i in range(WARM_UPS):
+            nc.tensor.matmul(unread[:], zeros[:], zeros[:], start=True, stop=True)
+
         identity = held.tile([P, P], BF16, name="identity")
         make_identity(nc, identity[:])
         base_rows = [held.tile([P, tokens], BF16, name=f"base_rows{a}") for a in range(blocks)]
@@ -50,9 +59,8 @@ def tile_scatter_matmul_kernel(tc, base, x, w, b, offs, out):
 
         for a in range(blocks):
             for e in range(experts):
-                columns = piece // PER_COLUMN
                 nc.tensor.matmul(
-                    windows[a][:].indirect(offsets[:, e * columns : (e + 1) * columns]),
+                    windows[a][:].indirect(offsets[:, e * piece_columns : (e + 1) * piece_columns]),
                     weights[:, e, a * P : (a + 1) * P],
                     moving[:, e * piece : (e + 1) * piece],
                     start=False,

@@ -9,7 +9,7 @@ GELU = mybir.ActivationFunctionType.Gelu_apprx_tanh
 P = 128
 PER_COLUMN = 16
 
-WARM_UPS = 16
+WARM_UPS = 12
 
 FLOPS = 2 * 128 * 256 * 256
 

@@ -37,17 +37,17 @@ def tile_scatter_matmul_kernel(tc, base, x, w, b, offs, out):
         identity = held.tile([P, P], BF16, name="identity")
         make_identity(nc, identity[:])
         base_rows = [held.tile([P, tokens], BF16, name=f"base_rows{a}") for a in range(blocks)]
-        nc.sync.dma_start(base_rows[0][:], base[0:P, :])
-        nc.scalar.dma_start(base_rows[1][:], base[P : 2 * P, :])
+        for a in range(blocks):
+            nc.sync.dma_start(base_rows[a][:], base[a * P : (a + 1) * P, :])
         offsets = held.tile([P, entries // PER_COLUMN], U16, name="offsets")
         nc.sync.dma_start(offsets[:], offs)
         moving = held.tile([P, entries], BF16, name="moving")
         nc.sync.dma_start(moving[:], x)
         weights = held.tile([P, experts, features], BF16, name="weights")
-        nc.scalar.dma_start(weights[:], w.rearrange("e k m -> k e m"))
+        nc.sync.dma_start(weights[:], w.rearrange("e k m -> k e m"))
         bias = held.tile([P, blocks], F32, name="bias")
         with nc.allow_non_contiguous_dma(reason="one float32 of the bias to a partition and block"):
-            nc.scalar.dma_start(bias[:], b.rearrange("(a p) o -> p (a o)", p=P))
+            nc.sync.dma_start(bias[:], b.rearrange("(a p) o -> p (a o)", p=P))
 
         scratch = held.tile([P, 1], F32, name="scratch")
         nc.vector.memset(scratch[:], 0.0)

@@ -35,7 +35,8 @@ def tile_scatter_matmul_kernel(tc, base, x, w, b, offs, out):
             nc.tensor.matmul(unread[:], zeros[:], zeros[:], start=True, stop=True)
 
         identity = held.tile([P, P], BF16, name="identity")
-        make_identity(nc, identity[:])
+        nc.vector.memset(identity[:], 0.0)
+        make_identity(nc, identity[:], nomemset=True)
         base_rows = [held.tile([P, tokens], BF16, name=f"base_rows{a}") for a in range(blocks)]
         for a in range(blocks):
             nc.sync.dma_start(base_rows[a][:], base[a * P : (a + 1) * P, :])

@@ -9,7 +9,8 @@ GELU = mybir.ActivationFunctionType.Gelu_apprx_tanh
 P = 128
 PER_COLUMN = 16
 
-WARM_UPS = 12
+WARM_UPS = 3
+REPEATS = 4
 
 FLOPS = 2 * 128 * 256 * 256
 
@@ -30,9 +31,11 @@ def tile_scatter_matmul_kernel(tc, base, x, w, b, offs, out):
     ):
         zeros = held.tile([P, P], BF16, name="zeros")
         nc.vector.memset(zeros[:], 0.0)
-        unread = banks.tile([P, P], F32, name="unread")
+        unread = banks.tile([P, REPEATS, P], F32, name="unread")
         for i in range(WARM_UPS):
-            nc.tensor.matmul(unread[:], zeros[:], zeros[:], start=True, stop=True)
+            nc.tensor.matmul(
+                unread[:], zeros[:], zeros[:].unsqueeze(1).to_broadcast([P, REPEATS, P]), start=True, stop=True
+            )
 
         identity = held.tile([P, P], BF16, name="identity")
         nc.vector.memset(identity[:], 0.0)
@@ -51,8 +54,7 @@ def tile_scatter_matmul_kernel(tc, base, x, w, b, offs, out):
             nc.sync.dma_start(bias[:], b.rearrange("(a p) o -> p (a o)", p=P))
 
         scratch = held.tile([P, 1], F32, name="scratch")
-        nc.vector.memset(scratch[:], 0.0)
-        nc.scalar.activation(scratch[:], scratch[:], GELU)
+        nc.scalar.activation(scratch[:], zeros[:, 0:1], GELU)
 
         windows = [banks.tile([P, tokens], F32, name=f"window{a}") for a in range(blocks)]
         for a in range(blocks):

@@ -43,12 +43,12 @@ def tile_scatter_matmul_kernel(tc, base, x, w, b, offs, out):
         base_rows = [held.tile([P, tokens], BF16, name=f"base_rows{a}") for a in range(blocks)]
         for a in range(blocks):
             nc.sync.dma_start(base_rows[a][:], base[a * P : (a + 1) * P, :])
-        offsets = held.tile([P, entries // PER_COLUMN], U16, name="offsets")
-        nc.sync.dma_start(offsets[:], offs)
-        moving = held.tile([P, entries], BF16, name="moving")
-        nc.sync.dma_start(moving[:], x)
         weights = held.tile([P, experts, features], BF16, name="weights")
         nc.sync.dma_start(weights[:], w.rearrange("e k m -> k e m"))
+        moving = held.tile([P, entries], BF16, name="moving")
+        nc.sync.dma_start(moving[:], x)
+        offsets = held.tile([P, entries // PER_COLUMN], U16, name="offsets")
+        nc.sync.dma_start(offsets[:], offs)
         bias = held.tile([P, blocks], F32, name="bias")
         with nc.allow_non_contiguous_dma(reason="one float32 of the bias to a partition and block"):
             nc.sync.dma_start(bias[:], b.rearrange("(a p) o -> p (a o)", p=P))

@@ -8,6 +8,7 @@ GELU = mybir.ActivationFunctionType.Gelu_apprx_tanh
 
 P = 128
 PER_COLUMN = 16
+BURST = 256
 
 WARM_UPS = 3
 REPEATS = 4
@@ -40,12 +41,12 @@ def tile_scatter_matmul_kernel(tc, base, x, w, b, offs, out):
         identity = held.tile([P, P], BF16, name="identity")
         nc.vector.memset(identity[:], 0.0)
         make_identity(nc, identity[:], nomemset=True)
-        base_rows = [held.tile([P, tokens], BF16, name=f"base_rows{a}") for a in range(blocks)]
+        base_rows = [held.tile([P, tokens], BF16, name=f"base_rows{a}", align_bytes=BURST) for a in range(blocks)]
         for a in range(blocks):
             nc.sync.dma_start(base_rows[a][:], base[a * P : (a + 1) * P, :])
-        weights = held.tile([P, experts, features], BF16, name="weights")
+        weights = held.tile([P, experts, features], BF16, name="weights", align_bytes=BURST)
         nc.sync.dma_start(weights[:], w.rearrange("e k m -> k e m"))
-        moving = held.tile([P, entries], BF16, name="moving")
+        moving = held.tile([P, entries], BF16, name="moving", align_bytes=BURST)
         nc.sync.dma_start(moving[:], x)
         offsets = held.tile([P, entries // PER_COLUMN], U16, name="offsets")
         nc.sync.dma_start(offsets[:], offs)
@@ -71,6 +72,6 @@ def tile_scatter_matmul_kernel(tc, base, x, w, b, offs, out):
                 )
 
         for a in range(blocks):
-            result = held.tile([P, tokens], F32, name=f"result{a}")
+            result = held.tile([P, tokens], F32, name=f"result{a}", align_bytes=BURST)
             nc.scalar.activation(result[:], windows[a][:], GELU, bias=bias[:, a : a + 1])
             nc.sync.dma_start(out[a * P : (a + 1) * P, :], result[:])

@@ -8,7 +8,7 @@ GELU = mybir.ActivationFunctionType.Gelu_apprx_tanh
 
 P = 128
 PER_COLUMN = 16
-BURST = 256
+BURST = 2048
 
 WARM_UPS = 3
 REPEATS = 4

import concourse.mybir as mybir
from concourse.masks import make_identity

BF16 = mybir.dt.bfloat16
F32 = mybir.dt.float32
U16 = mybir.dt.uint16
GELU = mybir.ActivationFunctionType.Gelu_apprx_tanh

P = 128
PER_COLUMN = 16
BURST = 2048

WARM_UPS = 3
REPEATS = 4

FLOPS = 2 * 128 * 256 * 256


def tile_scatter_matmul_kernel(tc, base, x, w, b, offs, out):
    nc = tc.nc
    features, tokens = base.shape
    contraction, entries = x.shape
    experts = w.shape[0]
    piece = entries // experts
    piece_columns = piece // PER_COLUMN
    blocks = features // P
    assert contraction == P

    with (
        tc.tile_pool(name="held", bufs=1) as held,
        tc.psum_pool(name="banks", bufs=1) as banks,
    ):
        zeros = held.tile([P, P], BF16, name="zeros")
        nc.vector.memset(zeros[:], 0.0)
        unread = banks.tile([P, REPEATS, P], F32, name="unread")
        for i in range(WARM_UPS):
            nc.tensor.matmul(
                unread[:], zeros[:], zeros[:].unsqueeze(1).to_broadcast([P, REPEATS, P]), start=True, stop=True
            )

        identity = held.tile([P, P], BF16, name="identity")
        nc.vector.memset(identity[:], 0.0)
        make_identity(nc, identity[:], nomemset=True)
        base_rows = [held.tile([P, tokens], BF16, name=f"base_rows{a}", align_bytes=BURST) for a in range(blocks)]
        for a in range(blocks):
            nc.sync.dma_start(base_rows[a][:], base[a * P : (a + 1) * P, :])
        weights = held.tile([P, experts, features], BF16, name="weights", align_bytes=BURST)
        nc.sync.dma_start(weights[:], w.rearrange("e k m -> k e m"))
        moving = held.tile([P, entries], BF16, name="moving", align_bytes=BURST)
        nc.sync.dma_start(moving[:], x)
        offsets = held.tile([P, entries // PER_COLUMN], U16, name="offsets")
        nc.sync.dma_start(offsets[:], offs)
        bias = held.tile([P, blocks], F32, name="bias")
        with nc.allow_non_contiguous_dma(reason="one float32 of the bias to a partition and block"):
            nc.sync.dma_start(bias[:], b.rearrange("(a p) o -> p (a o)", p=P))

        scratch = held.tile([P, 1], F32, name="scratch")
        nc.scalar.activation(scratch[:], zeros[:, 0:1], GELU)

        windows = [banks.tile([P, tokens], F32, name=f"window{a}") for a in range(blocks)]
        for a in range(blocks):
            nc.tensor.matmul(windows[a][:], identity[:], base_rows[a][:], start=True, stop=False)

        for a in range(blocks):
            for e in range(experts):
                nc.tensor.matmul(
                    windows[a][:].indirect(offsets[:, e * piece_columns : (e + 1) * piece_columns]),
                    weights[:, e, a * P : (a + 1) * P],
                    moving[:, e * piece : (e + 1) * piece],
                    start=False,
                    stop=(e == experts - 1),
                )

        for a in range(blocks):
            result = held.tile([P, tokens], F32, name=f"result{a}", align_bytes=BURST)
            nc.scalar.activation(result[:], windows[a][:], GELU, bias=bias[:, a : a + 1])
            nc.sync.dma_start(out[a * P : (a + 1) * P, :], result[:])
